import numpy as np, ml_dtypes
CORES = [12,28,44,60,3,19,35,51]
N = 8
C = 128
def setup_inputs(rng):
    x = 150 * rng.standard_normal((1, 128, C), dtype=np.float32) + 2 * rng.standard_normal((N, 128, C), dtype=np.float32)
    x = (x + rng.uniform(100, 300, (1, 128, C)) * (rng.random((1, 128, C)) < 0.7) * (rng.random((N, 128, C)) < 0.5)).astype(np.float32)
    return {"x": x}
def setup_inputs_trail(rng):
    d = setup_inputs(rng); x = d["x"].copy(); t = int(rng.integers(N))
    x[t] = np.delete(x, t, axis=0).max(axis=0) - rng.uniform(3.0, 20.0, x[t].shape).astype(np.float32)
    return {"x": x}
def reference(x):
    X = x.astype(np.float64)
    P = np.exp(X - X.max(axis=0))
    return {"y": (P / P.sum(axis=0)).astype(ml_dtypes.bfloat16)}

@@ -1,0 +1,141 @@
+from concourse.bass import DstId, RemoteDMATransfer
+from concourse.mybir import AluOpType, ActivationFunctionType
+
+N = 8
+P = 128
+C = 128
+SIM_CORES = 64
+K = 4
+W = C // K
+REP = 2
+BW = REP * W
+NP = N // REP
+
+SCRATCH = {
+    "xs": ("dram", [K, P, W], "float32"),
+    "ys": ("dram", [K, P, W], "bfloat16"),
+    "X": ("sbuf", [P, N * W], "float32"),
+    "m1a": ("sbuf", [P, 2 * W], "float32"),
+    "m2": ("sbuf", [P, 2 * W], "float32"),
+    "D": ("sbuf", [P, N * W], "float32"),
+    "Pb": ("sbuf", [P, N * W], "bfloat16"),
+    "Y": ("sbuf", [P, N * W], "bfloat16"),
+    "ones": ("sbuf", [P, P], "bfloat16"),
+    "ident": ("sbuf", [P, P], "bfloat16"),
+    "m1b": ("psum", [P, 512], "float32"),
+    "Mp": ("psum", [P, 512], "float32"),
+    "Sp": ("psum", [P, 512], "float32"),
+    "Rp": ("psum", [P, 512], "float32"),
+}
+SEMAPHORES = (["ld", "sent", "xarr", "yarr", "st", "v", "one", "idn", "pe"]
+              + ["d%d" % i for i in range(NP)] + ["e%d" % i for i in range(NP)])
+
+
+def _owners(T, topo):
+    ranks = list(T.cores)
+    cand = [c for c in range(SIM_CORES) if T.rank_of(c) is None
+            and all(topo.may_write(r, c) and topo.may_write(c, r) for r in ranks)]
+    owners = []
+    for r in ranks:
+        here = [c for c in cand if topo.chip(c) == topo.chip(r)]
+        same = [c for c in here if topo.die(c) == topo.die(r)]
+        if here:
+            owners.append((same or here)[0])
+    return ranks, owners
+
+
+def _split(topo, src, dsts):
+    allowed = topo.mask(src, dsts[0])
+    for d in dsts[1:]:
+        allowed &= topo.mask(src, d)
+    eng = [e for e in range(allowed.bit_length()) if (allowed >> e) & 1]
+    per = 1
+    while 2 * per * len(dsts) <= len(eng):
+        per *= 2
+    masks = [sum(1 << e for e in eng[i * per:(i + 1) * per]) for i in range(len(dsts))]
+    return per, masks
+
+
+def _fused(g, topo, src, items, remote_sem, local_sem):
+    per, masks = _split(topo, src, [d for d, _, _ in items])
+    trs = []
+    for (d, s, t), m in zip(items, masks):
+        rid, pid, _ = topo.addr(d)
+        trs.append(RemoteDMATransfer(dst_ids=[DstId(rid=rid, pnc=pid)], dma_engine_mask=m,
+                                     remote_sem=remote_sem, src=s, dst=t))
+    g.remote_dma_fused(trs, local_sem=local_sem)
+    return per * len(items)
+
+
+def _rank(g, core, T, topo, j, ranks, owners):
+    sem = T.sem
+    g.sync.dma_start(T.xs[:], T.x[:]).then_inc(sem.ld, 16)
+    g.wait_ge(sem.ld, 16)
+    left = _fused(g, topo, core, [(o, T.xs[k], T.X[:, j * W:(j + 1) * W]) for k, o in enumerate(owners)],
+                  sem.xarr, sem.sent)
+    g.sync.wait_ge(sem.yarr, sum(_split(topo, o, ranks)[0] for o in owners))
+    g.sync.dma_start(T.y[:], T.ys[:]).then_inc(sem.st, 16)
+    g.wait_ge(sem.sent, left)
+    g.sync.wait_ge(sem.st, 16)
+
+
+def _owner(g, core, T, topo, k, ranks, owners):
+    sem = T.sem
+    V, A, PE = g.vector, g.scalar, g.tensor
+    tt = V.tensor_tensor
+    nv = [0]
+
+    def done(ins):
+        ins.then_inc(sem.v, 1)
+        nv[0] += 1
+
+    def sync():
+        V.wait_ge(sem.v, nv[0])
+
+    def piece(t, i):
+        return t[:, i * BW:(i + 1) * BW]
+
+    V.memset(T.ones[:], 1.0).then_inc(sem.one, 1)
+    g.wait_ge(sem.one, 1)
+    g.affine_select(T.ident[:], T.ones[:], [[-1, P]], AluOpType.is_equal, 0.0, 0, 1).then_inc(sem.idn, 1)
+
+    V.wait_ge(sem.xarr, sum(_split(topo, r, owners)[0] for r in ranks))
+    done(tt(T.m1a[:], T.X[:, 0:2 * W], T.X[:, 4 * W:6 * W], AluOpType.max))
+    done(tt(T.m1b[:, 0:2 * W], T.X[:, 2 * W:4 * W], T.X[:, 6 * W:8 * W], AluOpType.max))
+    sync()
+    done(tt(T.m2[:], T.m1a[:], T.m1b[:, 0:2 * W], AluOpType.max))
+    sync()
+    for t in range(REP):
+        done(tt(T.Mp[:, t * W:(t + 1) * W], T.m2[:, 0:W], T.m2[:, W:2 * W], AluOpType.max))
+    sync()
+    for i in range(NP):
+        tt(piece(T.D, i), piece(T.X, i), T.Mp[:, 0:BW], AluOpType.subtract).then_inc(sem["d%d" % i], 1)
+    for i in range(NP):
+        A.wait_ge(sem["d%d" % i], 1)
+        A.activation(piece(T.Pb, i), piece(T.D, i), ActivationFunctionType.Exp).then_inc(sem["e%d" % i], 1)
+    PE.wait_ge(sem.idn, 1)
+    for i in range(NP):
+        PE.wait_ge(sem["e%d" % i], 1)
+        for j in range(i * REP, (i + 1) * REP):
+            mm = PE.matmul(T.Sp[:, 0:W], T.ident[:], T.Pb[:, j * W:(j + 1) * W], j == 0, j == N - 1)
+    mm.then_inc(sem.pe, 1)
+    V.wait_ge(sem.pe, 1)
+    done(V.reciprocal(T.Rp[:, 0:W], T.Sp[:, 0:W]))
+    sync()
+    for t in range(1, REP):
+        done(V.tensor_copy(T.Rp[:, t * W:(t + 1) * W], T.Rp[:, 0:W]))
+    sync()
+    for i in range(NP):
+        done(tt(piece(T.Y, i), piece(T.Pb, i), T.Rp[:, 0:BW], AluOpType.mult))
+    g.wait_ge(sem.v, nv[0])
+    left = _fused(g, topo, core, [(r, T.Y[:, j * W:(j + 1) * W], T.ys[k]) for j, r in enumerate(ranks)],
+                  sem.yarr, sem.sent)
+    g.wait_ge(sem.sent, left)
+
+
+def rank_program(g, core, T, topo):
+    ranks, owners = _owners(T, topo)
+    if core in ranks:
+        _rank(g, core, T, topo, ranks.index(core), ranks, owners)
+    elif core in owners:
+        _owner(g, core, T, topo, owners.index(core), ranks, owners)

@@ -10,6 +10,8 @@ W = C // K
 REP = 2
 BW = REP * W
 NP = N // REP
+PES = [0, 1, 2, 4, 6]
+VES = [3, 5, 7]
 
 SCRATCH = {
     "xs": ("dram", [K, P, W], "float32"),
@@ -20,14 +22,16 @@ SCRATCH = {
     "D": ("sbuf", [P, N * W], "float32"),
     "Pb": ("sbuf", [P, N * W], "bfloat16"),
     "Y": ("sbuf", [P, N * W], "bfloat16"),
-    "ones": ("sbuf", [P, P], "bfloat16"),
+    "pmi": ("sbuf", [P, P], "float32"),
+    "sq": ("sbuf", [P, P], "float32"),
     "ident": ("sbuf", [P, P], "bfloat16"),
+    "So": ("sbuf", [P, 4 * W], "float32"),
     "m1b": ("psum", [P, 512], "float32"),
     "Mp": ("psum", [P, 512], "float32"),
     "Sp": ("psum", [P, 512], "float32"),
     "Rp": ("psum", [P, 512], "float32"),
 }
-SEMAPHORES = (["ld", "sent", "xarr", "yarr", "st", "v", "one", "idn", "pe"]
+SEMAPHORES = (["ld", "sent", "xnear", "xfar", "yarr", "st", "v", "one", "sqd", "idn", "pe"]
               + ["d%d" % i for i in range(NP)] + ["e%d" % i for i in range(NP)])
 
 
@@ -44,6 +48,11 @@ def _owners(T, topo):
     return ranks, owners
 
 
+def _slots(topo, o, ranks):
+    near = [r for r in ranks if topo.chip(r) == topo.chip(o) or topo.same_plane(topo.chip(r), topo.chip(o))]
+    return near, [r for r in ranks if r not in near]
+
+
 def _split(topo, src, dsts):
     allowed = topo.mask(src, dsts[0])
     for d in dsts[1:]:
@@ -56,10 +65,10 @@ def _split(topo, src, dsts):
     return per, masks
 
 
-def _fused(g, topo, src, items, remote_sem, local_sem):
-    per, masks = _split(topo, src, [d for d, _, _ in items])
+def _fused(g, topo, src, items, local_sem):
+    per, masks = _split(topo, src, [it[0] for it in items])
     trs = []
-    for (d, s, t), m in zip(items, masks):
+    for (d, s, t, remote_sem), m in zip(items, masks):
         rid, pid, _ = topo.addr(d)
         trs.append(RemoteDMATransfer(dst_ids=[DstId(rid=rid, pnc=pid)], dma_engine_mask=m,
                                      remote_sem=remote_sem, src=s, dst=t))
@@ -67,12 +76,16 @@ def _fused(g, topo, src, items, remote_sem, local_sem):
     return per * len(items)
 
 
-def _rank(g, core, T, topo, j, ranks, owners):
+def _rank(g, core, T, topo, ranks, owners):
     sem = T.sem
     g.sync.dma_start(T.xs[:], T.x[:]).then_inc(sem.ld, 16)
     g.wait_ge(sem.ld, 16)
-    left = _fused(g, topo, core, [(o, T.xs[k], T.X[:, j * W:(j + 1) * W]) for k, o in enumerate(owners)],
-                  sem.xarr, sem.sent)
+    items = []
+    for k, o in enumerate(owners):
+        near, far = _slots(topo, o, ranks)
+        n = (near + far).index(core)
+        items.append((o, T.xs[k], T.X[:, n * W:(n + 1) * W], sem.xnear if core in near else sem.xfar))
+    left = _fused(g, topo, core, items, sem.sent)
     g.sync.wait_ge(sem.yarr, sum(_split(topo, o, ranks)[0] for o in owners))
     g.sync.dma_start(T.y[:], T.ys[:]).then_inc(sem.st, 16)
     g.wait_ge(sem.sent, left)
@@ -95,18 +108,26 @@ def _owner(g, core, T, topo, k, ranks, owners):
     def piece(t, i):
         return t[:, i * BW:(i + 1) * BW]
 
-    V.memset(T.ones[:], 1.0).then_inc(sem.one, 1)
-    g.wait_ge(sem.one, 1)
-    g.affine_select(T.ident[:], T.ones[:], [[-1, P]], AluOpType.is_equal, 0.0, 0, 1).then_inc(sem.idn, 1)
+    def slot(t, j):
+        return t[:, j * W:(j + 1) * W]
 
-    V.wait_ge(sem.xarr, sum(_split(topo, r, owners)[0] for r in ranks))
-    done(tt(T.m1a[:], T.X[:, 0:2 * W], T.X[:, 4 * W:6 * W], AluOpType.max))
-    done(tt(T.m1b[:, 0:2 * W], T.X[:, 2 * W:4 * W], T.X[:, 6 * W:8 * W], AluOpType.max))
+    near, far = _slots(topo, core, ranks)
+    slots = near + far
+    g.iota(T.pmi[:], [[-1, P]], 0, 1, allow_small_or_imprecise_dtypes=True).then_inc(sem.one, 1)
+    A.wait_ge(sem.one, 1)
+    A.activation(T.sq[:], T.pmi[:], ActivationFunctionType.Square).then_inc(sem.sqd, 1)
+    A.wait_ge(sem.sqd, 1)
+    A.activation(T.ident[:], T.sq[:], ActivationFunctionType.Exp, scale=-100.0).then_inc(sem.idn, 1)
+
+    V.wait_ge(sem.xnear, sum(_split(topo, r, owners)[0] for r in near))
+    done(tt(T.m1a[:], T.X[:, 0:2 * W], T.X[:, 2 * W:4 * W], AluOpType.max))
+    V.wait_ge(sem.xfar, sum(_split(topo, r, owners)[0] for r in far))
+    done(tt(T.m1b[:, 0:2 * W], T.X[:, 4 * W:6 * W], T.X[:, 6 * W:8 * W], AluOpType.max))
     sync()
     done(tt(T.m2[:], T.m1a[:], T.m1b[:, 0:2 * W], AluOpType.max))
     sync()
     for t in range(REP):
-        done(tt(T.Mp[:, t * W:(t + 1) * W], T.m2[:, 0:W], T.m2[:, W:2 * W], AluOpType.max))
+        done(tt(slot(T.Mp, t), T.m2[:, 0:W], T.m2[:, W:2 * W], AluOpType.max))
     sync()
     for i in range(NP):
         tt(piece(T.D, i), piece(T.X, i), T.Mp[:, 0:BW], AluOpType.subtract).then_inc(sem["d%d" % i], 1)
@@ -114,28 +135,36 @@ def _owner(g, core, T, topo, k, ranks, owners):
         A.wait_ge(sem["d%d" % i], 1)
         A.activation(piece(T.Pb, i), piece(T.D, i), ActivationFunctionType.Exp).then_inc(sem["e%d" % i], 1)
     PE.wait_ge(sem.idn, 1)
-    for i in range(NP):
-        PE.wait_ge(sem["e%d" % i], 1)
-        for j in range(i * REP, (i + 1) * REP):
-            mm = PE.matmul(T.Sp[:, 0:W], T.ident[:], T.Pb[:, j * W:(j + 1) * W], j == 0, j == N - 1)
+    for n, j in enumerate(PES):
+        PE.wait_ge(sem["e%d" % (j // REP)], 1)
+        mm = PE.matmul(T.Sp[:, 0:W], T.ident[:], slot(T.Pb, j), n == 0, n == len(PES) - 1)
     mm.then_inc(sem.pe, 1)
+    acc = slot(T.Pb, VES[0])
+    V.wait_ge(sem["e%d" % (VES[0] // REP)], 1)
+    for n, j in enumerate(VES[1:]):
+        V.wait_ge(sem["e%d" % (j // REP)], 1)
+        sync()
+        done(tt(slot(T.So, n), acc, slot(T.Pb, j), AluOpType.add))
+        acc = slot(T.So, n)
     V.wait_ge(sem.pe, 1)
-    done(V.reciprocal(T.Rp[:, 0:W], T.Sp[:, 0:W]))
+    sync()
+    done(tt(slot(T.So, 3), acc, T.Sp[:, 0:W], AluOpType.add))
+    sync()
+    done(V.reciprocal(T.Rp[:, 0:W], slot(T.So, 3)))
     sync()
     for t in range(1, REP):
-        done(V.tensor_copy(T.Rp[:, t * W:(t + 1) * W], T.Rp[:, 0:W]))
+        done(V.tensor_copy(slot(T.Rp, t), T.Rp[:, 0:W]))
     sync()
     for i in range(NP):
         done(tt(piece(T.Y, i), piece(T.Pb, i), T.Rp[:, 0:BW], AluOpType.mult))
     g.wait_ge(sem.v, nv[0])
-    left = _fused(g, topo, core, [(r, T.Y[:, j * W:(j + 1) * W], T.ys[k]) for j, r in enumerate(ranks)],
-                  sem.yarr, sem.sent)
+    left = _fused(g, topo, core, [(r, slot(T.Y, n), T.ys[k], sem.yarr) for n, r in enumerate(slots)], sem.sent)
     g.wait_ge(sem.sent, left)
 
 
 def rank_program(g, core, T, topo):
     ranks, owners = _owners(T, topo)
     if core in ranks:
-        _rank(g, core, T, topo, ranks.index(core), ranks, owners)
+        _rank(g, core, T, topo, ranks, owners)
     elif core in owners:
         _owner(g, core, T, topo, owners.index(core), ranks, owners)

@@ -7,32 +7,27 @@ C = 128
 SIM_CORES = 64
 K = 4
 W = C // K
-REP = 2
-BW = REP * W
-NP = N // REP
-PES = [0, 1, 2, 4, 6]
-VES = [3, 5, 7]
+H = N // 2
+BIG = 1.0e9
 
 SCRATCH = {
     "xs": ("dram", [K, P, W], "float32"),
     "ys": ("dram", [K, P, W], "bfloat16"),
     "X": ("sbuf", [P, N * W], "float32"),
-    "m1a": ("sbuf", [P, 2 * W], "float32"),
-    "m2": ("sbuf", [P, 2 * W], "float32"),
+    "mask": ("sbuf", [P, H * W], "float32"),
+    "m1": ("sbuf", [P, H * W], "float32"),
     "D": ("sbuf", [P, N * W], "float32"),
     "Pb": ("sbuf", [P, N * W], "bfloat16"),
     "Y": ("sbuf", [P, N * W], "bfloat16"),
     "pmi": ("sbuf", [P, P], "float32"),
     "sq": ("sbuf", [P, P], "float32"),
     "ident": ("sbuf", [P, P], "bfloat16"),
-    "So": ("sbuf", [P, 4 * W], "float32"),
-    "m1b": ("psum", [P, 512], "float32"),
-    "Mp": ("psum", [P, 512], "float32"),
+    "Ms": ("psum", [P, 512], "float32"),
     "Sp": ("psum", [P, 512], "float32"),
     "Rp": ("psum", [P, 512], "float32"),
 }
-SEMAPHORES = (["ld", "sent", "xnear", "xfar", "yarr", "st", "v", "one", "sqd", "idn", "pe"]
-              + ["d%d" % i for i in range(NP)] + ["e%d" % i for i in range(NP)])
+SEMAPHORES = (["ld", "sent", "xnear", "xfar", "yarr", "st", "v", "one", "sqd", "idn", "pe", "mk"]
+              + ["d%d" % i for i in range(N)] + ["e%d" % i for i in range(N)])
 
 
 def _owners(T, topo):
@@ -96,6 +91,7 @@ def _owner(g, core, T, topo, k, ranks, owners):
     sem = T.sem
     V, A, PE = g.vector, g.scalar, g.tensor
     tt = V.tensor_tensor
+    Exp = ActivationFunctionType.Exp
     nv = [0]
 
     def done(ins):
@@ -104,9 +100,6 @@ def _owner(g, core, T, topo, k, ranks, owners):
 
     def sync():
         V.wait_ge(sem.v, nv[0])
-
-    def piece(t, i):
-        return t[:, i * BW:(i + 1) * BW]
 
     def slot(t, j):
         return t[:, j * W:(j + 1) * W]
@@ -117,46 +110,36 @@ def _owner(g, core, T, topo, k, ranks, owners):
     A.wait_ge(sem.one, 1)
     A.activation(T.sq[:], T.pmi[:], ActivationFunctionType.Square).then_inc(sem.sqd, 1)
     A.wait_ge(sem.sqd, 1)
-    A.activation(T.ident[:], T.sq[:], ActivationFunctionType.Exp, scale=-100.0).then_inc(sem.idn, 1)
+    A.activation(T.ident[:], T.sq[:], Exp, scale=-100.0).then_inc(sem.idn, 1)
+    V.memset(T.mask[:], BIG).then_inc(sem.mk, 1)
+    V.wait_ge(sem.mk, 1)
+    V.memset(T.mask[:, 0:H * W:H], -BIG).then_inc(sem.mk, 1)
+    V.wait_ge(sem.mk, 2)
 
     V.wait_ge(sem.xnear, sum(_split(topo, r, owners)[0] for r in near))
-    done(tt(T.m1a[:], T.X[:, 0:2 * W], T.X[:, 2 * W:4 * W], AluOpType.max))
-    V.wait_ge(sem.xfar, sum(_split(topo, r, owners)[0] for r in far))
-    done(tt(T.m1b[:, 0:2 * W], T.X[:, 4 * W:6 * W], T.X[:, 6 * W:8 * W], AluOpType.max))
+    for i in range(H):
+        if 2 * i == len(near):
+            V.wait_ge(sem.xfar, sum(_split(topo, r, owners)[0] for r in far))
+        done(tt(T.m1[:, i:H * W:H], slot(T.X, 2 * i), slot(T.X, 2 * i + 1), AluOpType.max))
     sync()
-    done(tt(T.m2[:], T.m1a[:], T.m1b[:, 0:2 * W], AluOpType.max))
+    done(V.tensor_tensor_scan(T.Ms[:, 0:H * W], T.mask[:], T.m1[:], 0.0, AluOpType.min, AluOpType.max))
     sync()
-    for t in range(REP):
-        done(tt(slot(T.Mp, t), T.m2[:, 0:W], T.m2[:, W:2 * W], AluOpType.max))
-    sync()
-    for i in range(NP):
-        tt(piece(T.D, i), piece(T.X, i), T.Mp[:, 0:BW], AluOpType.subtract).then_inc(sem["d%d" % i], 1)
-    for i in range(NP):
-        A.wait_ge(sem["d%d" % i], 1)
-        A.activation(piece(T.Pb, i), piece(T.D, i), ActivationFunctionType.Exp).then_inc(sem["e%d" % i], 1)
+    M = T.Ms[:, H - 1:H * W:H]
+    for j in range(N):
+        tt(slot(T.D, j), slot(T.X, j), M, AluOpType.subtract).then_inc(sem["d%d" % j], 1)
+    for j in range(N):
+        A.wait_ge(sem["d%d" % j], 1)
+        A.activation(slot(T.Pb, j), slot(T.D, j), Exp).then_inc(sem["e%d" % j], 1)
     PE.wait_ge(sem.idn, 1)
-    for n, j in enumerate(PES):
-        PE.wait_ge(sem["e%d" % (j // REP)], 1)
-        mm = PE.matmul(T.Sp[:, 0:W], T.ident[:], slot(T.Pb, j), n == 0, n == len(PES) - 1)
+    for j in range(N):
+        PE.wait_ge(sem["e%d" % j], 1)
+        mm = PE.matmul(T.Sp[:, 0:W], T.ident[:], slot(T.Pb, j), j == 0, j == N - 1)
     mm.then_inc(sem.pe, 1)
-    acc = slot(T.Pb, VES[0])
-    V.wait_ge(sem["e%d" % (VES[0] // REP)], 1)
-    for n, j in enumerate(VES[1:]):
-        V.wait_ge(sem["e%d" % (j // REP)], 1)
-        sync()
-        done(tt(slot(T.So, n), acc, slot(T.Pb, j), AluOpType.add))
-        acc = slot(T.So, n)
     V.wait_ge(sem.pe, 1)
+    done(V.reciprocal(T.Rp[:, 0:W], T.Sp[:, 0:W]))
     sync()
-    done(tt(slot(T.So, 3), acc, T.Sp[:, 0:W], AluOpType.add))
-    sync()
-    done(V.reciprocal(T.Rp[:, 0:W], slot(T.So, 3)))
-    sync()
-    for t in range(1, REP):
-        done(V.tensor_copy(slot(T.Rp, t), T.Rp[:, 0:W]))
-    sync()
-    for i in range(NP):
-        done(tt(piece(T.Y, i), piece(T.Pb, i), T.Rp[:, 0:BW], AluOpType.mult))
+    for j in range(N):
+        done(tt(slot(T.Y, j), slot(T.Pb, j), T.Rp[:, 0:W], AluOpType.mult))
     g.wait_ge(sem.v, nv[0])
     left = _fused(g, topo, core, [(r, slot(T.Y, n), T.ys[k], sem.yarr) for n, r in enumerate(slots)], sem.sent)
     g.wait_ge(sem.sent, left)

@@ -9,25 +9,32 @@ K = 4
 W = C // K
 H = N // 2
 BIG = 1.0e9
+GROUPS = (1, 3, 3)
+HOME = 4
 
 SCRATCH = {
     "xs": ("dram", [K, P, W], "float32"),
     "ys": ("dram", [K, P, W], "bfloat16"),
+    "ph": ("sbuf", [P, W], "bfloat16"),
+    "rh": ("sbuf", [P, W], "float32"),
+    "yh": ("sbuf", [P, W], "bfloat16"),
     "X": ("sbuf", [P, N * W], "float32"),
     "mask": ("sbuf", [P, H * W], "float32"),
     "m1": ("sbuf", [P, H * W], "float32"),
     "D": ("sbuf", [P, N * W], "float32"),
     "Pb": ("sbuf", [P, N * W], "bfloat16"),
+    "Rs": ("sbuf", [P, W], "float32"),
     "Y": ("sbuf", [P, N * W], "bfloat16"),
     "pmi": ("sbuf", [P, P], "float32"),
     "sq": ("sbuf", [P, P], "float32"),
     "ident": ("sbuf", [P, P], "bfloat16"),
     "Ms": ("psum", [P, 512], "float32"),
     "Sp": ("psum", [P, 512], "float32"),
-    "Rp": ("psum", [P, 512], "float32"),
 }
-SEMAPHORES = (["ld", "sent", "xnear", "xfar", "yarr", "st", "v", "one", "sqd", "idn", "pe", "mk"]
-              + ["d%d" % i for i in range(N)] + ["e%d" % i for i in range(N)])
+SEMAPHORES = (["ld0", "ld1", "sent", "xnear", "xfar", "yarr", "st", "sth", "v", "one", "sqd", "idn", "pe", "mk",
+               "hp", "hr", "hy"]
+              + ["d%d" % i for i in range(N)] + ["e%d" % i for i in range(N)]
+              + ["y%d" % q for q in range(len(GROUPS))])
 
 
 def _owners(T, topo):
@@ -48,11 +55,15 @@ def _slots(topo, o, ranks):
     return near, [r for r in ranks if r not in near]
 
 
+def _bits(mask):
+    return [e for e in range(mask.bit_length()) if (mask >> e) & 1]
+
+
 def _split(topo, src, dsts):
     allowed = topo.mask(src, dsts[0])
     for d in dsts[1:]:
         allowed &= topo.mask(src, d)
-    eng = [e for e in range(allowed.bit_length()) if (allowed >> e) & 1]
+    eng = _bits(allowed)
     per = 1
     while 2 * per * len(dsts) <= len(eng):
         per *= 2
@@ -60,31 +71,59 @@ def _split(topo, src, dsts):
     return per, masks
 
 
-def _fused(g, topo, src, items, local_sem):
-    per, masks = _split(topo, src, [it[0] for it in items])
+def _returns(topo, o, ranks):
+    near, far = _slots(topo, o, ranks)
+    home = [r for r in near if topo.chip(r) == topo.chip(o)][0]
+    away = far + [r for r in near if r != home]
+    _, masks = _split(topo, o, away)
+    calls, at = [], 0
+    for n in GROUPS:
+        calls.append(list(zip(away[at:at + n], masks[at:at + n])))
+        at += n
+    hmask = sum(1 << e for e in _bits(topo.mask(o, home) & ~topo.mask(o, away[0]))[:HOME])
+    return home, hmask, calls
+
+
+def _fused(g, topo, items, local_sem):
     trs = []
-    for (d, s, t, remote_sem), m in zip(items, masks):
+    for d, m, s, t, remote_sem in items:
         rid, pid, _ = topo.addr(d)
         trs.append(RemoteDMATransfer(dst_ids=[DstId(rid=rid, pnc=pid)], dma_engine_mask=m,
                                      remote_sem=remote_sem, src=s, dst=t))
     g.remote_dma_fused(trs, local_sem=local_sem)
-    return per * len(items)
+    return sum(len(_bits(it[1])) for it in items)
 
 
 def _rank(g, core, T, topo, ranks, owners):
     sem = T.sem
-    g.sync.dma_start(T.xs[:], T.x[:]).then_inc(sem.ld, 16)
-    g.wait_ge(sem.ld, 16)
+    R = P // K
+    g.sync.dma_start(T.xs[0:K // 2], T.x[0:P // 2, :]).then_inc(sem.ld0, 16)
+    g.scalar.dma_start(T.xs[K // 2:K], T.x[P // 2:P, :]).then_inc(sem.ld1, 16)
     items = []
-    for k, o in enumerate(owners):
+    for (k, o), m in zip(enumerate(owners), _split(topo, core, owners)[1]):
         near, far = _slots(topo, o, ranks)
         n = (near + far).index(core)
-        items.append((o, T.xs[k], T.X[:, n * W:(n + 1) * W], sem.xnear if core in near else sem.xfar))
-    left = _fused(g, topo, core, items, sem.sent)
-    g.sync.wait_ge(sem.yarr, sum(_split(topo, o, ranks)[0] for o in owners))
-    g.sync.dma_start(T.y[:], T.ys[:]).then_inc(sem.st, 16)
+        items.append((o, m, T.xs[k], T.X[:, n * W:(n + 1) * W], sem.xnear if core in near else sem.xfar))
+    g.wait_ge(sem.ld0, 16)
+    left = _fused(g, topo, items[0:K // 2], sem.sent)
+    g.wait_ge(sem.ld1, 16)
+    left += _fused(g, topo, items[K // 2:K], sem.sent)
+    mine = [k for k, o in enumerate(owners) if _returns(topo, o, ranks)[0] == core]
+    g.sync.wait_ge(sem.yarr, sum(len(_bits(m)) for o in owners for c in _returns(topo, o, ranks)[2]
+                                 for r, m in c if r == core))
+    runs = [(0, K)] if not mine else [(a, b) for a, b in ((0, mine[0]), (mine[0] + 1, K)) if a < b]
+    for a, b in runs:
+        g.sync.dma_start(T.y[a * R:b * R, :], T.ys[a:b]).then_inc(sem.st, 16)
+    if mine:
+        n = len(_bits(_returns(topo, owners[mine[0]], ranks)[1]))
+        g.vector.wait_ge(sem.hp, n)
+        g.vector.wait_ge(sem.hr, n)
+        g.vector.tensor_tensor(T.yh[:], T.ph[:], T.rh[:], AluOpType.mult).then_inc(sem.hy, 1)
+        g.scalar.wait_ge(sem.hy, 1)
+        g.scalar.dma_start(T.y[mine[0] * R:(mine[0] + 1) * R, :], T.yh[:]).then_inc(sem.sth, 16)
+        g.scalar.wait_ge(sem.sth, 16)
     g.wait_ge(sem.sent, left)
-    g.sync.wait_ge(sem.st, 16)
+    g.sync.wait_ge(sem.st, 16 * len(runs))
 
 
 def _owner(g, core, T, topo, k, ranks, owners):
@@ -106,6 +145,9 @@ def _owner(g, core, T, topo, k, ranks, owners):
 
     near, far = _slots(topo, core, ranks)
     slots = near + far
+    home, hmask, calls = _returns(topo, core, ranks)
+    h = slots.index(home)
+    order = [h] + [j for j in range(N) if j != h]
     g.iota(T.pmi[:], [[-1, P]], 0, 1, allow_small_or_imprecise_dtypes=True).then_inc(sem.one, 1)
     A.wait_ge(sem.one, 1)
     A.activation(T.sq[:], T.pmi[:], ActivationFunctionType.Square).then_inc(sem.sqd, 1)
@@ -125,23 +167,30 @@ def _owner(g, core, T, topo, k, ranks, owners):
     done(V.tensor_tensor_scan(T.Ms[:, 0:H * W], T.mask[:], T.m1[:], 0.0, AluOpType.min, AluOpType.max))
     sync()
     M = T.Ms[:, H - 1:H * W:H]
-    for j in range(N):
+    for j in order:
         tt(slot(T.D, j), slot(T.X, j), M, AluOpType.subtract).then_inc(sem["d%d" % j], 1)
-    for j in range(N):
+    for j in order:
         A.wait_ge(sem["d%d" % j], 1)
         A.activation(slot(T.Pb, j), slot(T.D, j), Exp).then_inc(sem["e%d" % j], 1)
     PE.wait_ge(sem.idn, 1)
-    for j in range(N):
+    for n, j in enumerate(order):
         PE.wait_ge(sem["e%d" % j], 1)
-        mm = PE.matmul(T.Sp[:, 0:W], T.ident[:], slot(T.Pb, j), j == 0, j == N - 1)
+        mm = PE.matmul(T.Sp[:, 0:W], T.ident[:], slot(T.Pb, j), n == 0, n == N - 1)
     mm.then_inc(sem.pe, 1)
+    g.wait_ge(sem["e%d" % h], 1)
+    left = _fused(g, topo, [(home, hmask, slot(T.Pb, h), T.ph[:], sem.hp)], sem.sent)
     V.wait_ge(sem.pe, 1)
-    done(V.reciprocal(T.Rp[:, 0:W], T.Sp[:, 0:W]))
+    done(V.reciprocal(T.Rs[:], T.Sp[:, 0:W]))
     sync()
-    for j in range(N):
-        done(tt(slot(T.Y, j), slot(T.Pb, j), T.Rp[:, 0:W], AluOpType.mult))
+    for q, call in enumerate(calls):
+        for r, _ in call:
+            n = slots.index(r)
+            tt(slot(T.Y, n), slot(T.Pb, n), T.Rs[:], AluOpType.mult).then_inc(sem["y%d" % q], 1)
     g.wait_ge(sem.v, nv[0])
-    left = _fused(g, topo, core, [(r, slot(T.Y, n), T.ys[k], sem.yarr) for n, r in enumerate(slots)], sem.sent)
+    left += _fused(g, topo, [(home, hmask, T.Rs[:], T.rh[:], sem.hr)], sem.sent)
+    for q, call in enumerate(calls):
+        g.wait_ge(sem["y%d" % q], len(call))
+        left += _fused(g, topo, [(r, m, slot(T.Y, slots.index(r)), T.ys[k], sem.yarr) for r, m in call], sem.sent)
     g.wait_ge(sem.sent, left)
 
 

@@ -8,13 +8,14 @@ SIM_CORES = 64
 K = 4
 W = C // K
 H = N // 2
+MW = H * W * K // N
 BIG = 1.0e9
-GROUPS = (1, 3, 3)
-HOME = 4
+GROUPS = (1, 2, 2, 2)
 
 SCRATCH = {
     "xs": ("dram", [K, P, W], "float32"),
     "ys": ("dram", [K, P, W], "bfloat16"),
+    "mh": ("sbuf", [P, MW], "float32"),
     "ph": ("sbuf", [P, W], "bfloat16"),
     "rh": ("sbuf", [P, W], "float32"),
     "yh": ("sbuf", [P, W], "bfloat16"),
@@ -31,7 +32,7 @@ SCRATCH = {
     "Ms": ("psum", [P, 512], "float32"),
     "Sp": ("psum", [P, 512], "float32"),
 }
-SEMAPHORES = (["ld0", "ld1", "sent", "xnear", "xfar", "yarr", "st", "sth", "v", "one", "sqd", "idn", "pe", "mk",
+SEMAPHORES = (["ld0", "ld1", "sent", "xnear", "xfar", "yarr", "st", "sth", "v", "one", "sqd", "idn", "pe", "mk", "mm",
                "hp", "hr", "hy"]
               + ["d%d" % i for i in range(N)] + ["e%d" % i for i in range(N)]
               + ["y%d" % q for q in range(len(GROUPS))])
@@ -71,17 +72,22 @@ def _split(topo, src, dsts):
     return per, masks
 
 
+def _ahead(topo, r, ranks, owners):
+    i = ranks.index(r)
+    return owners[i % K], i // K, sum(_split(topo, r, owners)[1])
+
+
 def _returns(topo, o, ranks):
     near, far = _slots(topo, o, ranks)
     home = [r for r in near if topo.chip(r) == topo.chip(o)][0]
     away = far + [r for r in near if r != home]
-    _, masks = _split(topo, o, away)
     calls, at = [], 0
     for n in GROUPS:
-        calls.append(list(zip(away[at:at + n], masks[at:at + n])))
+        calls.append(list(zip(away[at:at + n], _split(topo, o, away[at:at + n])[1])))
         at += n
-    hmask = sum(1 << e for e in _bits(topo.mask(o, home) & ~topo.mask(o, away[0]))[:HOME])
-    return home, hmask, calls
+    pmask = topo.mask(o, home)
+    hmask = pmask & ~topo.mask(o, away[0])
+    return home, pmask, hmask, calls
 
 
 def _fused(g, topo, items, local_sem):
@@ -99,25 +105,30 @@ def _rank(g, core, T, topo, ranks, owners):
     R = P // K
     g.sync.dma_start(T.xs[0:K // 2], T.x[0:P // 2, :]).then_inc(sem.ld0, 16)
     g.scalar.dma_start(T.xs[K // 2:K], T.x[P // 2:P, :]).then_inc(sem.ld1, 16)
+    for s in range(H):
+        g.vector.memset(T.mh[:, s:MW:H], -BIG if s == 0 else BIG).then_inc(sem.mm, 1)
+    mo, part, mmask = _ahead(topo, core, ranks, owners)
+    g.wait_ge(sem.mm, H)
+    left = _fused(g, topo, [(mo, mmask, T.mh[:], T.mask[:, part * MW:(part + 1) * MW], sem.mk)], sem.sent)
     items = []
     for (k, o), m in zip(enumerate(owners), _split(topo, core, owners)[1]):
         near, far = _slots(topo, o, ranks)
         n = (near + far).index(core)
         items.append((o, m, T.xs[k], T.X[:, n * W:(n + 1) * W], sem.xnear if core in near else sem.xfar))
     g.wait_ge(sem.ld0, 16)
-    left = _fused(g, topo, items[0:K // 2], sem.sent)
+    left += _fused(g, topo, items[0:K // 2], sem.sent)
     g.wait_ge(sem.ld1, 16)
     left += _fused(g, topo, items[K // 2:K], sem.sent)
     mine = [k for k, o in enumerate(owners) if _returns(topo, o, ranks)[0] == core]
-    g.sync.wait_ge(sem.yarr, sum(len(_bits(m)) for o in owners for c in _returns(topo, o, ranks)[2]
+    g.sync.wait_ge(sem.yarr, sum(len(_bits(m)) for o in owners for c in _returns(topo, o, ranks)[3]
                                  for r, m in c if r == core))
     runs = [(0, K)] if not mine else [(a, b) for a, b in ((0, mine[0]), (mine[0] + 1, K)) if a < b]
     for a, b in runs:
         g.sync.dma_start(T.y[a * R:b * R, :], T.ys[a:b]).then_inc(sem.st, 16)
     if mine:
-        n = len(_bits(_returns(topo, owners[mine[0]], ranks)[1]))
-        g.vector.wait_ge(sem.hp, n)
-        g.vector.wait_ge(sem.hr, n)
+        _, pmask, hmask, _ = _returns(topo, owners[mine[0]], ranks)
+        g.vector.wait_ge(sem.hp, len(_bits(pmask)))
+        g.vector.wait_ge(sem.hr, len(_bits(hmask)))
         g.vector.tensor_tensor(T.yh[:], T.ph[:], T.rh[:], AluOpType.mult).then_inc(sem.hy, 1)
         g.scalar.wait_ge(sem.hy, 1)
         g.scalar.dma_start(T.y[mine[0] * R:(mine[0] + 1) * R, :], T.yh[:]).then_inc(sem.sth, 16)
@@ -145,7 +156,7 @@ def _owner(g, core, T, topo, k, ranks, owners):
 
     near, far = _slots(topo, core, ranks)
     slots = near + far
-    home, hmask, calls = _returns(topo, core, ranks)
+    home, pmask, hmask, calls = _returns(topo, core, ranks)
     h = slots.index(home)
     order = [h] + [j for j in range(N) if j != h]
     g.iota(T.pmi[:], [[-1, P]], 0, 1, allow_small_or_imprecise_dtypes=True).then_inc(sem.one, 1)
@@ -153,16 +164,14 @@ def _owner(g, core, T, topo, k, ranks, owners):
     A.activation(T.sq[:], T.pmi[:], ActivationFunctionType.Square).then_inc(sem.sqd, 1)
     A.wait_ge(sem.sqd, 1)
     A.activation(T.ident[:], T.sq[:], Exp, scale=-100.0).then_inc(sem.idn, 1)
-    V.memset(T.mask[:], BIG).then_inc(sem.mk, 1)
-    V.wait_ge(sem.mk, 1)
-    V.memset(T.mask[:, 0:H * W:H], -BIG).then_inc(sem.mk, 1)
-    V.wait_ge(sem.mk, 2)
 
     V.wait_ge(sem.xnear, sum(_split(topo, r, owners)[0] for r in near))
     for i in range(H):
         if 2 * i == len(near):
             V.wait_ge(sem.xfar, sum(_split(topo, r, owners)[0] for r in far))
         done(tt(T.m1[:, i:H * W:H], slot(T.X, 2 * i), slot(T.X, 2 * i + 1), AluOpType.max))
+    V.wait_ge(sem.mk, sum(len(_bits(_ahead(topo, r, ranks, owners)[2])) for r in ranks
+                          if _ahead(topo, r, ranks, owners)[0] == core))
     sync()
     done(V.tensor_tensor_scan(T.Ms[:, 0:H * W], T.mask[:], T.m1[:], 0.0, AluOpType.min, AluOpType.max))
     sync()
@@ -178,7 +187,7 @@ def _owner(g, core, T, topo, k, ranks, owners):
         mm = PE.matmul(T.Sp[:, 0:W], T.ident[:], slot(T.Pb, j), n == 0, n == N - 1)
     mm.then_inc(sem.pe, 1)
     g.wait_ge(sem["e%d" % h], 1)
-    left = _fused(g, topo, [(home, hmask, slot(T.Pb, h), T.ph[:], sem.hp)], sem.sent)
+    left = _fused(g, topo, [(home, pmask, slot(T.Pb, h), T.ph[:], sem.hp)], sem.sent)
     V.wait_ge(sem.pe, 1)
     done(V.reciprocal(T.Rs[:], T.Sp[:, 0:W]))
     sync()
@@ -186,11 +195,12 @@ def _owner(g, core, T, topo, k, ranks, owners):
         for r, _ in call:
             n = slots.index(r)
             tt(slot(T.Y, n), slot(T.Pb, n), T.Rs[:], AluOpType.mult).then_inc(sem["y%d" % q], 1)
-    g.wait_ge(sem.v, nv[0])
-    left += _fused(g, topo, [(home, hmask, T.Rs[:], T.rh[:], sem.hr)], sem.sent)
     for q, call in enumerate(calls):
         g.wait_ge(sem["y%d" % q], len(call))
         left += _fused(g, topo, [(r, m, slot(T.Y, slots.index(r)), T.ys[k], sem.yarr) for r, m in call], sem.sent)
+        if q == 0:
+            g.wait_ge(sem.v, nv[0])
+            left += _fused(g, topo, [(home, hmask, T.Rs[:], T.rh[:], sem.hr)], sem.sent)
     g.wait_ge(sem.sent, left)
 
 

from concourse.bass import DstId, RemoteDMATransfer
from concourse.mybir import AluOpType, ActivationFunctionType

N = 8
P = 128
C = 128
SIM_CORES = 64
K = 4
W = C // K
H = N // 2
MW = H * W * K // N
BIG = 1.0e9
GROUPS = (1, 2, 2, 2)

SCRATCH = {
    "xs": ("dram", [K, P, W], "float32"),
    "ys": ("dram", [K, P, W], "bfloat16"),
    "mh": ("sbuf", [P, MW], "float32"),
    "ph": ("sbuf", [P, W], "bfloat16"),
    "rh": ("sbuf", [P, W], "float32"),
    "yh": ("sbuf", [P, W], "bfloat16"),
    "X": ("sbuf", [P, N * W], "float32"),
    "mask": ("sbuf", [P, H * W], "float32"),
    "m1": ("sbuf", [P, H * W], "float32"),
    "D": ("sbuf", [P, N * W], "float32"),
    "Pb": ("sbuf", [P, N * W], "bfloat16"),
    "Rs": ("sbuf", [P, W], "float32"),
    "Y": ("sbuf", [P, N * W], "bfloat16"),
    "pmi": ("sbuf", [P, P], "float32"),
    "sq": ("sbuf", [P, P], "float32"),
    "ident": ("sbuf", [P, P], "bfloat16"),
    "Ms": ("psum", [P, 512], "float32"),
    "Sp": ("psum", [P, 512], "float32"),
}
SEMAPHORES = (["ld0", "ld1", "sent", "xnear", "xfar", "yarr", "st", "sth", "v", "one", "sqd", "idn", "pe", "mk", "mm",
               "hp", "hr", "hy"]
              + ["d%d" % i for i in range(N)] + ["e%d" % i for i in range(N)]
              + ["y%d" % q for q in range(len(GROUPS))])


def _owners(T, topo):
    ranks = list(T.cores)
    cand = [c for c in range(SIM_CORES) if T.rank_of(c) is None
            and all(topo.may_write(r, c) and topo.may_write(c, r) for r in ranks)]
    owners = []
    for r in ranks:
        here = [c for c in cand if topo.chip(c) == topo.chip(r)]
        same = [c for c in here if topo.die(c) == topo.die(r)]
        if here:
            owners.append((same or here)[0])
    return ranks, owners


def _slots(topo, o, ranks):
    near = [r for r in ranks if topo.chip(r) == topo.chip(o) or topo.same_plane(topo.chip(r), topo.chip(o))]
    return near, [r for r in ranks if r not in near]


def _bits(mask):
    return [e for e in range(mask.bit_length()) if (mask >> e) & 1]


def _split(topo, src, dsts):
    allowed = topo.mask(src, dsts[0])
    for d in dsts[1:]:
        allowed &= topo.mask(src, d)
    eng = _bits(allowed)
    per = 1
    while 2 * per * len(dsts) <= len(eng):
        per *= 2
    masks = [sum(1 << e for e in eng[i * per:(i + 1) * per]) for i in range(len(dsts))]
    return per, masks


def _ahead(topo, r, ranks, owners):
    i = ranks.index(r)
    return owners[i % K], i // K, sum(_split(topo, r, owners)[1])


def _returns(topo, o, ranks):
    near, far = _slots(topo, o, ranks)
    home = [r for r in near if topo.chip(r) == topo.chip(o)][0]
    away = far + [r for r in near if r != home]
    calls, at = [], 0
    for n in GROUPS:
        calls.append(list(zip(away[at:at + n], _split(topo, o, away[at:at + n])[1])))
        at += n
    pmask = topo.mask(o, home)
    hmask = pmask & ~topo.mask(o, away[0])
    return home, pmask, hmask, calls


def _fused(g, topo, items, local_sem):
    trs = []
    for d, m, s, t, remote_sem in items:
        rid, pid, _ = topo.addr(d)
        trs.append(RemoteDMATransfer(dst_ids=[DstId(rid=rid, pnc=pid)], dma_engine_mask=m,
                                     remote_sem=remote_sem, src=s, dst=t))
    g.remote_dma_fused(trs, local_sem=local_sem)
    return sum(len(_bits(it[1])) for it in items)


def _rank(g, core, T, topo, ranks, owners):
    sem = T.sem
    R = P // K
    g.sync.dma_start(T.xs[0:K // 2], T.x[0:P // 2, :]).then_inc(sem.ld0, 16)
    g.scalar.dma_start(T.xs[K // 2:K], T.x[P // 2:P, :]).then_inc(sem.ld1, 16)
    for s in range(H):
        g.vector.memset(T.mh[:, s:MW:H], -BIG if s == 0 else BIG).then_inc(sem.mm, 1)
    mo, part, mmask = _ahead(topo, core, ranks, owners)
    g.wait_ge(sem.mm, H)
    left = _fused(g, topo, [(mo, mmask, T.mh[:], T.mask[:, part * MW:(part + 1) * MW], sem.mk)], sem.sent)
    items = []
    for (k, o), m in zip(enumerate(owners), _split(topo, core, owners)[1]):
        near, far = _slots(topo, o, ranks)
        n = (near + far).index(core)
        items.append((o, m, T.xs[k], T.X[:, n * W:(n + 1) * W], sem.xnear if core in near else sem.xfar))
    g.wait_ge(sem.ld0, 16)
    left += _fused(g, topo, items[0:K // 2], sem.sent)
    g.wait_ge(sem.ld1, 16)
    left += _fused(g, topo, items[K // 2:K], sem.sent)
    mine = [k for k, o in enumerate(owners) if _returns(topo, o, ranks)[0] == core]
    g.sync.wait_ge(sem.yarr, sum(len(_bits(m)) for o in owners for c in _returns(topo, o, ranks)[3]
                                 for r, m in c if r == core))
    runs = [(0, K)] if not mine else [(a, b) for a, b in ((0, mine[0]), (mine[0] + 1, K)) if a < b]
    for a, b in runs:
        g.sync.dma_start(T.y[a * R:b * R, :], T.ys[a:b]).then_inc(sem.st, 16)
    if mine:
        _, pmask, hmask, _ = _returns(topo, owners[mine[0]], ranks)
        g.vector.wait_ge(sem.hp, len(_bits(pmask)))
        g.vector.wait_ge(sem.hr, len(_bits(hmask)))
        g.vector.tensor_tensor(T.yh[:], T.ph[:], T.rh[:], AluOpType.mult).then_inc(sem.hy, 1)
        g.scalar.wait_ge(sem.hy, 1)
        g.scalar.dma_start(T.y[mine[0] * R:(mine[0] + 1) * R, :], T.yh[:]).then_inc(sem.sth, 16)
        g.scalar.wait_ge(sem.sth, 16)
    g.wait_ge(sem.sent, left)
    g.sync.wait_ge(sem.st, 16 * len(runs))


def _owner(g, core, T, topo, k, ranks, owners):
    sem = T.sem
    V, A, PE = g.vector, g.scalar, g.tensor
    tt = V.tensor_tensor
    Exp = ActivationFunctionType.Exp
    nv = [0]

    def done(ins):
        ins.then_inc(sem.v, 1)
        nv[0] += 1

    def sync():
        V.wait_ge(sem.v, nv[0])

    def slot(t, j):
        return t[:, j * W:(j + 1) * W]

    near, far = _slots(topo, core, ranks)
    slots = near + far
    home, pmask, hmask, calls = _returns(topo, core, ranks)
    h = slots.index(home)
    order = [h] + [j for j in range(N) if j != h]
    g.iota(T.pmi[:], [[-1, P]], 0, 1, allow_small_or_imprecise_dtypes=True).then_inc(sem.one, 1)
    A.wait_ge(sem.one, 1)
    A.activation(T.sq[:], T.pmi[:], ActivationFunctionType.Square).then_inc(sem.sqd, 1)
    A.wait_ge(sem.sqd, 1)
    A.activation(T.ident[:], T.sq[:], Exp, scale=-100.0).then_inc(sem.idn, 1)

    V.wait_ge(sem.xnear, sum(_split(topo, r, owners)[0] for r in near))
    for i in range(H):
        if 2 * i == len(near):
            V.wait_ge(sem.xfar, sum(_split(topo, r, owners)[0] for r in far))
        done(tt(T.m1[:, i:H * W:H], slot(T.X, 2 * i), slot(T.X, 2 * i + 1), AluOpType.max))
    V.wait_ge(sem.mk, sum(len(_bits(_ahead(topo, r, ranks, owners)[2])) for r in ranks
                          if _ahead(topo, r, ranks, owners)[0] == core))
    sync()
    done(V.tensor_tensor_scan(T.Ms[:, 0:H * W], T.mask[:], T.m1[:], 0.0, AluOpType.min, AluOpType.max))
    sync()
    M = T.Ms[:, H - 1:H * W:H]
    for j in order:
        tt(slot(T.D, j), slot(T.X, j), M, AluOpType.subtract).then_inc(sem["d%d" % j], 1)
    for j in order:
        A.wait_ge(sem["d%d" % j], 1)
        A.activation(slot(T.Pb, j), slot(T.D, j), Exp).then_inc(sem["e%d" % j], 1)
    PE.wait_ge(sem.idn, 1)
    for n, j in enumerate(order):
        PE.wait_ge(sem["e%d" % j], 1)
        mm = PE.matmul(T.Sp[:, 0:W], T.ident[:], slot(T.Pb, j), n == 0, n == N - 1)
    mm.then_inc(sem.pe, 1)
    g.wait_ge(sem["e%d" % h], 1)
    left = _fused(g, topo, [(home, pmask, slot(T.Pb, h), T.ph[:], sem.hp)], sem.sent)
    V.wait_ge(sem.pe, 1)
    done(V.reciprocal(T.Rs[:], T.Sp[:, 0:W]))
    sync()
    for q, call in enumerate(calls):
        for r, _ in call:
            n = slots.index(r)
            tt(slot(T.Y, n), slot(T.Pb, n), T.Rs[:], AluOpType.mult).then_inc(sem["y%d" % q], 1)
    for q, call in enumerate(calls):
        g.wait_ge(sem["y%d" % q], len(call))
        left += _fused(g, topo, [(r, m, slot(T.Y, slots.index(r)), T.ys[k], sem.yarr) for r, m in call], sem.sent)
        if q == 0:
            g.wait_ge(sem.v, nv[0])
            left += _fused(g, topo, [(home, hmask, T.Rs[:], T.rh[:], sem.hr)], sem.sent)
    g.wait_ge(sem.sent, left)


def rank_program(g, core, T, topo):
    ranks, owners = _owners(T, topo)
    if core in ranks:
        _rank(g, core, T, topo, ranks, owners)
    elif core in owners:
        _owner(g, core, T, topo, owners.index(core), ranks, owners)
